import numpy as np
import ml_dtypes


def mxq(x, axis, fmt="e4m3"):
    dtype, down = {"e4m3": (ml_dtypes.float8_e4m3fn, 7), "e5m2": (ml_dtypes.float8_e5m2, 14)}[fmt]
    v = np.moveaxis(np.asarray(x, np.float32).astype(ml_dtypes.bfloat16).astype(np.float64), axis, -1)
    blocks = v.reshape(v.shape[:-1] + (-1, 32))
    amax = np.abs(blocks).max(-1, keepdims=True)
    byte = np.maximum(np.where(amax > 0, np.frexp(amax)[1] - 1 + 127, 0) - down, 1)
    scale = np.exp2(byte - 127.0)
    codes = (blocks / scale).astype(np.float32).astype(dtype).astype(np.float64)
    return np.moveaxis((codes * scale).reshape(v.shape), -1, axis)


WIDE = False


def mx_kscale(k):
    if not WIDE:
        return np.ones(k)
    levels = np.array([10, -10, 5, -5, 0])
    if k % 512:
        return np.exp2(np.random.permutation(np.resize(levels, k // 32))).repeat(32)
    a = np.empty((k // 512, 16))
    for p in range(k // 512):
        a[p, :8] = np.random.permutation(np.resize(levels, 8))
        for g in range(8):
            far = levels[np.abs(levels - a[p, g]) >= 10]
            a[p, g + 8] = far[np.random.randint(len(far))]
    return np.exp2(a.ravel()).repeat(32)


def f64(x):
    return np.asarray(x).astype(np.float64)


def striped(idx):
    return np.tile(np.asarray(idx).reshape(-1, 16).T, (8, 1)).astype(np.uint16)


def unstriped(offs):
    return offs[:16].T.reshape(-1).astype(np.int64)


E2M1 = np.array([0.0, 0.5, 1.0, 1.5, 2.0, 3.0, 4.0, 6.0, -0.0, -0.5, -1.0, -1.5, -2.0, -3.0, -4.0, -6.0])


def pack_weight(w, fmt):
    k, n = w.shape
    w = f64(np.asarray(w, np.float32).astype(ml_dtypes.bfloat16)).reshape(k // 32, 32, n)
    amax = np.abs(w).max(1)
    if fmt == "e4m3":
        byte = np.frexp(amax)[1] - 1 + 127 - 7
    else:
        mant, ex = np.frexp(amax / 6.0)
        byte = np.where(mant > 0.5, ex, ex - 1) + 127
    byte = np.clip(np.where(amax > 0, byte, 1), 1, 254)
    scaled = (w * np.exp2(127.0 - byte)[:, None, :]).reshape(k, n).astype(np.float32)
    by_word = np.ascontiguousarray(scaled.reshape(k // 512, 128, 4, n).transpose(0, 1, 3, 2))
    if fmt == "e4m3":
        words = by_word.astype(ml_dtypes.float8_e4m3fn).view(np.uint8)
    else:
        c = by_word.astype(ml_dtypes.float4_e2m1fn).view(np.uint8) & 0xF
        words = (c[..., 0::2] | (c[..., 1::2] << 4)).reshape(k // 512, 128, 2 * n)
    return np.ascontiguousarray(words), np.ascontiguousarray(byte.astype(np.uint8).reshape(k // 512, 16, n))


def unpack_weight(words, scales, fmt):
    g, _, n = scales.shape
    words = np.ascontiguousarray(words).reshape(g, 128, n, -1)
    if fmt == "e4m3":
        vals = words.view(ml_dtypes.float8_e4m3fn).astype(np.float64)
    else:
        nib = np.empty((g, 128, n, 4), np.uint8)
        nib[..., 0::2] = words & 0xF
        nib[..., 1::2] = words >> 4
        vals = E2M1[nib]
    vals = vals * np.repeat(np.exp2(scales.astype(np.float64) - 127.0), 8, axis=1)[..., None]
    return vals.transpose(0, 1, 3, 2).reshape(g * 512, n)


def bf(x):
    return np.asarray(x, np.float32).astype(ml_dtypes.bfloat16)


def planes(Y):
    r, m = Y.shape
    b = f64(bf(Y)).reshape(r // 32, 32, m)
    amax = np.abs(b).max(1)
    byte = np.clip(np.where(amax > 0, np.frexp(amax)[1] - 1 + 127 - 7, 1), 1, 254)
    codes = (b * np.exp2(127.0 - byte)[:, None, :]).reshape(r, m).astype(np.float32).astype(ml_dtypes.float8_e4m3fn).view(np.uint8)
    words = codes.reshape(r // 512, 128, 4, m).transpose(0, 1, 3, 2)
    return np.ascontiguousarray(words), np.ascontiguousarray(byte.astype(np.uint8).reshape(r // 512, 16, m))


D, E, T, I, Q, G = 512, 512, 2048, 512, 256, 32


def setup_inputs():
    n = np.random.standard_normal
    idx = np.random.permutation(T)[:I]
    fd = mx_kscale(D)
    fi = mx_kscale(I)
    ti = np.ones(T)
    ti[idx] = fi
    keysp = pack_weight(n((D, T)) / fd[:, None], "e2m1")
    return {
        "query": (n((D, Q)) * 0.7 / np.sqrt(D) * fd[:, None]).astype(np.float32),
        "dquery": (n((D, Q)) * 1.0 / np.sqrt(D) * fd[:, None]).astype(np.float32),
        "keys_words": keysp[0],
        "keys_scales": keysp[1],
        "reserve": (np.random.uniform(1.0, 8.0, (I, 1))).astype(np.float32),
        "os": (np.random.uniform(0.1, 0.4, (I, 1)) * fi[:, None]).astype(np.float32),
        "vals": (n((E, T)) / ti).astype(np.float32),
        "offs": striped(idx),
    }


def reference(query, dquery, keys_words, keys_scales, reserve, os, vals, offs):
    idx = unstriped(offs)
    keysu = unpack_weight(keys_words, keys_scales, "e2m1")
    keysidxg = keysu[:, idx]
    queryq = mxq(f64(query), 0, "e4m3")
    a = keysidxg.T @ queryq
    dqueryq = mxq(f64(dquery), 0, "e4m3")
    ta = keysidxg.T @ dqueryq
    p = np.exp(a)
    s = 1.0 / (p.reshape(I, G, Q // G).sum(axis=2) + f64(reserve))
    sr = np.repeat(s, Q // G, axis=1)
    tp = ta * p
    ts = tp.reshape(I, G, Q // G).sum(axis=2) * (-1.0) / np.square(p.reshape(I, G, Q // G).sum(axis=2) + f64(reserve))
    tsr = np.repeat(ts, Q // G, axis=1)
    tw = tp * sr + tsr * p
    wo1 = tw * f64(os)
    vt1 = f64(vals)[:, idx].T
    vt1q = mxq(vt1, 0, "e4m3")
    wo1q = mxq(wo1, 0, "e4m3")
    o = vt1q.T @ wo1q
    words, scales = planes(o)
    return o, words, scales

@@ -1,0 +1,202 @@
+from contextlib import ExitStack
+
+import concourse.mybir as mybir
+from concourse.masks import make_identity
+
+D, E, T, I, Q, G = 512, 512, 2048, 512, 256, 32
+FLOPS = 2 * D * I * Q * 2 + 2 * I * E * Q
+
+F32 = mybir.dt.float32
+BF16 = mybir.dt.bfloat16
+I32 = mybir.dt.int32
+U32 = mybir.dt.uint32
+U16 = mybir.dt.uint16
+U8 = mybir.dt.uint8
+FP8X4 = mybir.dt.float8_e4m3fn_x4
+FP4X4 = mybir.dt.float4_e2m1fn_x4
+MULT = mybir.AluOpType.mult
+SUB = mybir.AluOpType.subtract
+EXP = mybir.ActivationFunctionType.Exp
+
+P = 128
+PACK = 4
+TEAM = Q // G
+HALVES = 2
+HG = G // HALVES
+
+
+def tile_attend_ttteamshares_pl_kernel(tc, query, dquery, keys_words, keys_scales, reserve, factor, vals, offs,
+                                        out_0, out_1, out_2):
+    nc = tc.nc
+    with ExitStack() as ctx:
+        held = ctx.enter_context(tc.tile_pool(name="held", bufs=1))
+        psum = ctx.enter_context(tc.psum_pool(name="psum", bufs=2))
+
+        def sb(name, shape, dtype, tag=None):
+            return held.tile(shape, dtype, name=name, tag=tag or name, align_bytes=64)
+
+        def bank(name, tag, shape):
+            return psum.tile(shape, F32, name=name, tag=tag)
+
+        offsets = held.tile([P, I // 16], U16, name="offsets")
+        key_pool = sb("key_pool", [P, T], U16)
+        key_scale_pool = sb("key_scale_pool", [P, T], U8)
+        nc.gpsimd.memset(key_scale_pool[:].bitcast(I32), 0)
+        nc.sync.dma_start(offsets[:], offs)
+        for quad in range(4):
+            nc.sync.dma_start(key_scale_pool[:].bitcast(I32)[32 * quad : 32 * quad + 4, :],
+                              keys_scales[0].bitcast(I32)[4 * quad : 4 * quad + 4, :])
+        nc.sync.dma_start(key_pool[:].bitcast(I32), keys_words[0].bitcast(I32))
+        q_raw = [sb("q_raw%d" % n, [P, PACK, Q], F32) for n in range(2)]
+        for n, src in enumerate((query, dquery)):
+            nc.sync.dma_start(q_raw[n][:], src.rearrange("(p j) q -> p j q", j=PACK))
+        slot_reserve = sb("slot_reserve", [P, PACK], F32)
+        slot_factor = sb("slot_factor", [P, PACK], F32)
+        nc.sync.dma_start(slot_reserve[:], reserve.rearrange("(p t) o -> p (t o)", t=PACK))
+        nc.sync.dma_start(slot_factor[:], factor.rearrange("(p t) o -> p (t o)", t=PACK))
+        val_rows = vals.rearrange("(p j) t -> j p t", j=PACK)
+        val_pool = [sb("val_pool%d" % j, [P, T], F32) for j in range(PACK)]
+        for j in range(PACK):
+            nc.sync.dma_start(val_pool[j][:], val_rows[j])
+
+        zeros = sb("zeros", [P, 8], F32)
+        nc.gpsimd.memset(zeros[:], 0.0)
+        warm = sb("warm", [P, 8], F32)
+        nc.scalar.activation(warm[:], zeros[:], EXP)
+        identity = sb("identity", [P, P], F32)
+        make_identity(nc, identity[:])
+        reserve_wide = sb("reserve_wide", [P, G, PACK], F32)
+        nc.gpsimd.tensor_copy(reserve_wide[:], slot_reserve[:].unsqueeze(1).to_broadcast([P, G, PACK]))
+
+        key_listed = sb("key_listed", [P, I], U16)
+        key_words = sb("key_words", [P, PACK, P], U16)
+        scale_listed = sb("scale_listed", [P, I], U8)
+        key_scales = sb("key_scales", [P, PACK, P], U8)
+        nc.vector.tensor_copy(scale_listed[:], key_scale_pool[:].indirect(offsets[:]))
+        nc.vector.tensor_copy(key_listed[:], key_pool[:].indirect(offsets[:]))
+        nc.vector.tensor_copy(key_scales[:], scale_listed[:].rearrange("p (s t) -> p t s", t=PACK))
+        nc.vector.tensor_copy(key_words[:], key_listed[:].rearrange("p (s t) -> p t s", t=PACK))
+
+        def interleave(copy, name, raw, cols):
+            width = cols.stop - cols.start
+            grouped = sb(name, [P, width, PACK], BF16)
+            copy(grouped[:].rearrange("p (c i) j -> p c j i", i=4),
+                 raw[:, :, cols].rearrange("p j (c i) -> p c j i", i=4))
+            return grouped
+
+        def quantize(name, grouped):
+            width = grouped.shape[1]
+            codes = sb(name + "_codes", [P, width], U32)
+            scales = sb(name + "_scales", [P, width], U8)
+            nc.vector.quantize_mx(codes[:].bitcast(FP8X4), scales[:], grouped[:].rearrange("p q j -> p (q j)"))
+            return codes, scales
+
+        def scores(name, tag, codes, scales):
+            acc = bank(name, tag, [P, PACK, P])
+            for t in range(PACK):
+                nc.tensor.matmul_mx(out=acc[:, t, :], lhsT=key_words[:, t, :].bitcast(FP4X4),
+                                    lhsT_scale=key_scales[:, t, :], rhs=codes.bitcast(FP8X4),
+                                    rhs_scale=scales, start=True, stop=True)
+            return acc[:].rearrange("p t (g r) -> p r g t", r=TEAM)
+
+        half_cols = [slice(P * h, P * (h + 1)) for h in range(HALVES)]
+        q_bf = [interleave(nc.scalar.copy, "q_bf%d" % h, q_raw[0], half_cols[h]) for h in range(HALVES)]
+        q_mx = [quantize("q0", q_bf[0])]
+        dq_bf = interleave(nc.vector.tensor_copy, "dq_bf", q_raw[1], slice(0, Q))
+        q_mx.append(quantize("q1", q_bf[1]))
+        dq_codes, dq_scales = quantize("dq", dq_bf)
+        a_banks = [scores("score%d" % h, "score", q_mx[h][0][:], q_mx[h][1][:]) for h in range(HALVES)]
+        ta_banks = [scores("tangent%d" % h, "tangent", dq_codes[:, half_cols[h]], dq_scales[:, half_cols[h]])
+                    for h in range(HALVES)]
+
+        val_codes = [sb("val_codes%d" % j, [P, P], U32) for j in range(PACK)]
+        val_scales = [sb("val_scales%d" % j, [P, P], U8) for j in range(PACK)]
+        val_bf = [sb("val_bf%d" % j, [P, P, PACK], BF16) for j in range(PACK)]
+
+        def turn_values(j):
+            listed = sb("val_listed%d" % j, [P, I], BF16, tag=("dq_codes", "reserve_wide", "weight", "mean")[j])
+            nc.vector.tensor_copy(listed[:], val_pool[j][:].indirect(offsets[:]))
+            pairs = listed[:].bitcast(F32)
+            turned = bank("turned%d" % j, "turned", [P, 2, P])
+            for u in range(2):
+                nc.tensor.transpose(turned[:, u, :], pairs[:, u : 2 * P : 2], identity[:])
+            nc.scalar.copy(val_bf[j][:].bitcast(F32), turned[:].rearrange("p u e -> p e u"))
+
+        def quantize_values(j):
+            nc.vector.quantize_mx(val_codes[j][:].bitcast(FP8X4), val_scales[j][:],
+                                  val_bf[j][:].rearrange("p e t -> p (e t)"))
+
+        def team_sums(name, slabs):
+            turned = bank(name + "_turned", "sums", [P, P])
+            for n, slab in enumerate(slabs):
+                nc.tensor.matmul(turned[:], lhsT=slab, rhs=identity[:], is_transpose=True,
+                                 start=(n == 0), stop=(n == len(slabs) - 1))
+            turned_sb = sb(name + "_turned_sb", [P, P], F32)
+            nc.scalar.copy(turned_sb[:], turned[:])
+            sums = bank(name, "sums", [P, P])
+            nc.tensor.transpose(sums[:], turned_sb[:], identity[:])
+            return sums
+
+        def slabs_of(tile):
+            return [tile[:, r].rearrange("p h g t -> p (h g t)") for r in range(TEAM)]
+
+        shape5 = [P, TEAM, HALVES, HG, PACK]
+        p_exp = sb("p_exp", shape5, F32)
+        for h in range(HALVES):
+            nc.scalar.activation(p_exp[:, :, h], a_banks[h], EXP)
+        den = team_sums("den", slabs_of(p_exp) + [reserve_wide[:].rearrange("p g t -> p (g t)")])
+        tp = sb("tp", shape5, F32)
+        for h in range(HALVES):
+            nc.vector.tensor_tensor(tp[:, :, h], ta_banks[h], p_exp[:, :, h], MULT)
+        turn_values(0)
+        tp_sum = team_sums("tp_sum", slabs_of(tp))
+        share = sb("share", [P, P], F32)
+        nc.vector.reciprocal(share[:], den[:])
+        quantize_values(0)
+        weight = sb("weight", [P, P], F32)
+        nc.vector.tensor_tensor(weight[:].rearrange("p (g t) -> p g t", t=PACK),
+                                share[:].rearrange("p (g t) -> p g t", t=PACK),
+                                slot_factor[:].unsqueeze(1).to_broadcast([P, G, PACK]), MULT)
+        mean = sb("mean", [P, HALVES, HG, PACK], F32)
+        nc.vector.tensor_tensor(mean[:].rearrange("p h g t -> p (h g t)"), tp_sum[:], share[:], MULT)
+        turn_values(1)
+        scaled = sb("scaled", [P, TEAM, P], F32)
+        nc.vector.tensor_tensor(scaled[:], p_exp[:].rearrange("p r h g t -> p r (h g t)"),
+                                weight[:].unsqueeze(1).to_broadcast([P, TEAM, P]), MULT)
+        centred = sb("centred", shape5, F32)
+        for h in range(HALVES):
+            nc.vector.tensor_tensor(centred[:, :, h], ta_banks[h],
+                                    mean[:, h].unsqueeze(1).to_broadcast([P, TEAM, HG, PACK]), SUB)
+        quantize_values(1)
+        turn_values(2)
+        turn_values(3)
+        quantize_values(2)
+        w_bf = [sb("w_bf%d" % h, [P, TEAM * HG, PACK], BF16) for h in range(HALVES)]
+        for h in range(HALVES):
+            nc.vector.tensor_tensor(w_bf[h][:].rearrange("p (r g) t -> p r (g t)", r=TEAM),
+                                    centred[:, :, h].rearrange("p r g t -> p r (g t)"),
+                                    scaled[:, :, HG * PACK * h : HG * PACK * (h + 1)], MULT)
+        quantize_values(3)
+        w_mx = [quantize("w%d" % h, w_bf[h]) for h in range(HALVES)]
+
+        result = [sb("result%d" % h, [P, PACK, P], F32) for h in range(HALVES)]
+        result_bf = sb("result_bf", [P, Q, PACK], BF16)
+        out_codes = sb("out_codes", [P, Q], U32)
+        out_scales = sb("out_scales", [P, Q], U8)
+        out_rows = out_0.rearrange("(p j) q -> p j q", j=PACK)
+        for h in range(HALVES):
+            acc = bank("out%d" % h, "score", [P, PACK, P])
+            for j in range(PACK):
+                nc.tensor.matmul_mx(out=acc[:, j, :], lhsT=val_codes[j][:].bitcast(FP8X4),
+                                    lhsT_scale=val_scales[j][:], rhs=w_mx[h][0][:].bitcast(FP8X4),
+                                    rhs_scale=w_mx[h][1][:], start=True, stop=True)
+            nc.vector.tensor_copy(result_bf[:, half_cols[h], :].rearrange("p (g r) j -> p g r j", r=TEAM),
+                                  acc[:].rearrange("p j (r g) -> p g r j", r=TEAM))
+            nc.scalar.copy(result[h][:].rearrange("p j (g r) -> p j g r", r=TEAM),
+                           acc[:].rearrange("p j (r g) -> p j g r", r=TEAM))
+            nc.scalar.dma_start(out_rows[:, :, half_cols[h]], result[h][:])
+        nc.vector.quantize_mx(out_codes[:].bitcast(FP8X4), out_scales[:], result_bf[:].rearrange("p q j -> p (q j)"))
+        nc.sync.dma_start(out_1[0].rearrange("p c r -> p (c r)").bitcast(I32), out_codes[:].bitcast(I32))
+        for quad in range(4):
+            nc.sync.dma_start(out_2[0].bitcast(I32)[4 * quad : 4 * quad + 4, :],
+                              out_scales[:].bitcast(I32)[32 * quad : 32 * quad + 4, :])

@@ -16,6 +16,7 @@ FP8X4 = mybir.dt.float8_e4m3fn_x4
 FP4X4 = mybir.dt.float4_e2m1fn_x4
 MULT = mybir.AluOpType.mult
 SUB = mybir.AluOpType.subtract
+COPY = mybir.ActivationFunctionType.Copy
 EXP = mybir.ActivationFunctionType.Exp
 
 P = 128
@@ -30,7 +31,7 @@ def tile_attend_ttteamshares_pl_kernel(tc, query, dquery, keys_words, keys_scale
     nc = tc.nc
     with ExitStack() as ctx:
         held = ctx.enter_context(tc.tile_pool(name="held", bufs=1))
-        psum = ctx.enter_context(tc.psum_pool(name="psum", bufs=2))
+        psum = ctx.enter_context(tc.psum_pool(name="psum", bufs=1))
 
         def sb(name, shape, dtype, tag=None):
             return held.tile(shape, dtype, name=name, tag=tag or name, align_bytes=64)
@@ -65,8 +66,9 @@ def tile_attend_ttteamshares_pl_kernel(tc, query, dquery, keys_words, keys_scale
         nc.scalar.activation(warm[:], zeros[:], EXP)
         identity = sb("identity", [P, P], F32)
         make_identity(nc, identity[:])
-        reserve_wide = sb("reserve_wide", [P, G, PACK], F32)
-        nc.gpsimd.tensor_copy(reserve_wide[:], slot_reserve[:].unsqueeze(1).to_broadcast([P, G, PACK]))
+        reserve_wide = sb("reserve_wide", [P, 2, HG, PACK], F32)
+        nc.gpsimd.memset(reserve_wide[:, 1], 0.0)
+        nc.gpsimd.tensor_copy(reserve_wide[:, 0], slot_reserve[:].unsqueeze(1).to_broadcast([P, HG, PACK]))
 
         key_listed = sb("key_listed", [P, I], U16)
         key_words = sb("key_words", [P, PACK, P], U16)
@@ -100,103 +102,145 @@ def tile_attend_ttteamshares_pl_kernel(tc, query, dquery, keys_words, keys_scale
             return acc[:].rearrange("p t (g r) -> p r g t", r=TEAM)
 
         half_cols = [slice(P * h, P * (h + 1)) for h in range(HALVES)]
-        q_bf = [interleave(nc.scalar.copy, "q_bf%d" % h, q_raw[0], half_cols[h]) for h in range(HALVES)]
-        q_mx = [quantize("q0", q_bf[0])]
-        dq_bf = interleave(nc.vector.tensor_copy, "dq_bf", q_raw[1], slice(0, Q))
-        q_mx.append(quantize("q1", q_bf[1]))
+        q_bf = interleave(nc.scalar.copy, "q_bf", q_raw[0], slice(0, Q))
+        dq_bf = interleave(nc.scalar.copy, "dq_bf", q_raw[1], slice(0, Q))
+        q_codes, q_scales = quantize("q", q_bf)
         dq_codes, dq_scales = quantize("dq", dq_bf)
-        a_banks = [scores("score%d" % h, "score", q_mx[h][0][:], q_mx[h][1][:]) for h in range(HALVES)]
-        ta_banks = [scores("tangent%d" % h, "tangent", dq_codes[:, half_cols[h]], dq_scales[:, half_cols[h]])
-                    for h in range(HALVES)]
 
-        val_codes = [sb("val_codes%d" % j, [P, P], U32) for j in range(PACK)]
-        val_scales = [sb("val_scales%d" % j, [P, P], U8) for j in range(PACK)]
-        val_bf = [sb("val_bf%d" % j, [P, P, PACK], BF16) for j in range(PACK)]
+        early = PACK - 1
+        early_bf = sb("early_bf", [P, early * P, PACK], BF16)
+        last_bf = sb("last_bf", [P, P, PACK], BF16)
+        val_bf = [early_bf[:, P * j : P * (j + 1), :] for j in range(early)] + [last_bf[:]]
 
-        def turn_values(j):
-            listed = sb("val_listed%d" % j, [P, I], BF16, tag=("dq_codes", "reserve_wide", "weight", "mean")[j])
-            nc.vector.tensor_copy(listed[:], val_pool[j][:].indirect(offsets[:]))
+        def gather_values(j):
+            listed = sb("val_listed%d" % j, [P, I], BF16)
+            if j < early:
+                nc.vector.tensor_copy(listed[:], val_pool[j][:].indirect(offsets[:]))
+            else:
+                rounded = sb("val_rounded", [P, T], BF16)
+                for c0 in range(0, T, I):
+                    nc.scalar.activation(rounded[:, c0 : c0 + I], val_pool[j][:, c0 : c0 + I], COPY)
+                nc.scalar.activation(listed[:], rounded[:].indirect(offsets[:]), COPY)
+            return listed
+
+        def turn_values(j, listed, tag):
             pairs = listed[:].bitcast(F32)
-            turned = bank("turned%d" % j, "turned", [P, 2, P])
+            turned = bank("turned%d" % j, tag, [P, 2, P])
             for u in range(2):
                 nc.tensor.transpose(turned[:, u, :], pairs[:, u : 2 * P : 2], identity[:])
-            nc.scalar.copy(val_bf[j][:].bitcast(F32), turned[:].rearrange("p u e -> p e u"))
+            nc.scalar.copy(val_bf[j].bitcast(F32), turned[:].rearrange("p u e -> p e u"))
 
-        def quantize_values(j):
-            nc.vector.quantize_mx(val_codes[j][:].bitcast(FP8X4), val_scales[j][:],
-                                  val_bf[j][:].rearrange("p e t -> p (e t)"))
+        val_mx = {}
 
-        def team_sums(name, slabs):
-            turned = bank(name + "_turned", "sums", [P, P])
+        def quantize_values(name, planes_in, tag):
+            codes = sb(name + "_codes", [P, len(planes_in) * P], U32, tag=tag)
+            scales = sb(name + "_scales", [P, len(planes_in) * P], U8)
+            for n, j in enumerate(planes_in):
+                cols = slice(P * n, P * (n + 1))
+                nc.vector.quantize_mx(codes[:, cols].bitcast(FP8X4), scales[:, cols],
+                                      val_bf[j].rearrange("p e t -> p (e t)"))
+                val_mx[j] = (codes[:, cols], scales[:, cols])
+
+        def exp_and_change(h):
+            a_bank = scores("score%d" % h, "score%d" % h, q_codes[:, half_cols[h]], q_scales[:, half_cols[h]])
+            ta_bank = scores("tangent%d" % h, "tangent%d" % h, dq_codes[:, half_cols[h]], dq_scales[:, half_cols[h]])
+            both = sb("both%d" % h, [P, TEAM, 2, HG, PACK], F32, tag="val_pool0" if h == 0 else None)
+            nc.scalar.activation(both[:, :, 0], a_bank, EXP)
+            nc.vector.tensor_tensor(both[:, :, 1], ta_bank, both[:, :, 0], MULT)
+            return both, ta_bank
+
+        def team_sums(h, both):
+            slabs = [both[:, r].rearrange("p k g t -> p (k g t)") for r in range(TEAM)]
+            slabs.append(reserve_wide[:].rearrange("p k g t -> p (k g t)"))
+            turned = bank("sums_turned%d" % h, "sums_turned%d" % h, [P, P])
             for n, slab in enumerate(slabs):
                 nc.tensor.matmul(turned[:], lhsT=slab, rhs=identity[:], is_transpose=True,
                                  start=(n == 0), stop=(n == len(slabs) - 1))
-            turned_sb = sb(name + "_turned_sb", [P, P], F32)
+            turned_sb = sb("sums_turned_sb%d" % h, [P, P], F32)
             nc.scalar.copy(turned_sb[:], turned[:])
-            sums = bank(name, "sums", [P, P])
-            nc.tensor.transpose(sums[:], turned_sb[:], identity[:])
+            sums = bank("sums%d" % h, ("sums0", "sums_turned0")[h], [P, 2, HG, PACK])
+            nc.tensor.transpose(sums[:].rearrange("p k g t -> p (k g t)"), turned_sb[:], identity[:])
             return sums
 
-        def slabs_of(tile):
-            return [tile[:, r].rearrange("p h g t -> p (h g t)") for r in range(TEAM)]
+        team_shape = [P, HG, PACK]
+        row_shape = [P, TEAM, HG, PACK]
 
-        shape5 = [P, TEAM, HALVES, HG, PACK]
-        p_exp = sb("p_exp", shape5, F32)
-        for h in range(HALVES):
-            nc.scalar.activation(p_exp[:, :, h], a_banks[h], EXP)
-        den = team_sums("den", slabs_of(p_exp) + [reserve_wide[:].rearrange("p g t -> p (g t)")])
-        tp = sb("tp", shape5, F32)
-        for h in range(HALVES):
-            nc.vector.tensor_tensor(tp[:, :, h], ta_banks[h], p_exp[:, :, h], MULT)
-        turn_values(0)
-        tp_sum = team_sums("tp_sum", slabs_of(tp))
-        share = sb("share", [P, P], F32)
-        nc.vector.reciprocal(share[:], den[:])
-        quantize_values(0)
-        weight = sb("weight", [P, P], F32)
-        nc.vector.tensor_tensor(weight[:].rearrange("p (g t) -> p g t", t=PACK),
-                                share[:].rearrange("p (g t) -> p g t", t=PACK),
-                                slot_factor[:].unsqueeze(1).to_broadcast([P, G, PACK]), MULT)
-        mean = sb("mean", [P, HALVES, HG, PACK], F32)
-        nc.vector.tensor_tensor(mean[:].rearrange("p h g t -> p (h g t)"), tp_sum[:], share[:], MULT)
-        turn_values(1)
-        scaled = sb("scaled", [P, TEAM, P], F32)
-        nc.vector.tensor_tensor(scaled[:], p_exp[:].rearrange("p r h g t -> p r (h g t)"),
-                                weight[:].unsqueeze(1).to_broadcast([P, TEAM, P]), MULT)
-        centred = sb("centred", shape5, F32)
-        for h in range(HALVES):
-            nc.vector.tensor_tensor(centred[:, :, h], ta_banks[h],
-                                    mean[:, h].unsqueeze(1).to_broadcast([P, TEAM, HG, PACK]), SUB)
-        quantize_values(1)
-        turn_values(2)
-        turn_values(3)
-        quantize_values(2)
-        w_bf = [sb("w_bf%d" % h, [P, TEAM * HG, PACK], BF16) for h in range(HALVES)]
-        for h in range(HALVES):
-            nc.vector.tensor_tensor(w_bf[h][:].rearrange("p (r g) t -> p r (g t)", r=TEAM),
-                                    centred[:, :, h].rearrange("p r g t -> p r (g t)"),
-                                    scaled[:, :, HG * PACK * h : HG * PACK * (h + 1)], MULT)
-        quantize_values(3)
-        w_mx = [quantize("w%d" % h, w_bf[h]) for h in range(HALVES)]
+        def share_of(h, sums):
+            share = sb("share%d" % h, team_shape, F32, tag=("val_pool2", "weight0")[h])
+            nc.vector.reciprocal(share[:], sums[:, 0])
+            return share
 
-        result = [sb("result%d" % h, [P, PACK, P], F32) for h in range(HALVES)]
-        result_bf = sb("result_bf", [P, Q, PACK], BF16)
+        def weight_and_mean(h, sums, share):
+            weight = sb("weight%d" % h, team_shape, F32)
+            nc.vector.tensor_tensor(weight[:], share[:], slot_factor[:].unsqueeze(1).to_broadcast(team_shape), MULT)
+            mean = sb("mean%d" % h, team_shape, F32)
+            nc.vector.tensor_tensor(mean[:], sums[:, 1], share[:], MULT)
+            return weight, mean
+
+        def factors(h, both, ta_bank, weight, mean):
+            scaled = sb("scaled%d" % h, row_shape, F32)
+            nc.vector.tensor_tensor(scaled[:], both[:, :, 0], weight[:].unsqueeze(1).to_broadcast(row_shape), MULT)
+            centred = sb("centred%d" % h, row_shape, F32)
+            nc.vector.tensor_tensor(centred[:], ta_bank, mean[:].unsqueeze(1).to_broadcast(row_shape), SUB)
+            return scaled, centred
+
+        def product(h, scaled, centred, tag):
+            w_bf = sb("w_bf%d" % h, [P, TEAM * HG, PACK], BF16, tag=tag)
+            nc.vector.tensor_tensor(w_bf[:].rearrange("p n t -> p (n t)"), centred[:].rearrange("p r g t -> p (r g t)"),
+                                    scaled[:].rearrange("p r g t -> p (r g t)"), MULT)
+            return w_bf
+
         out_codes = sb("out_codes", [P, Q], U32)
         out_scales = sb("out_scales", [P, Q], U8)
         out_rows = out_0.rearrange("(p j) q -> p j q", j=PACK)
-        for h in range(HALVES):
-            acc = bank("out%d" % h, "score", [P, PACK, P])
+
+        def read_values(h, w_codes, w_scales, round_copy):
+            acc = bank("out%d" % h, "score%d" % h, [P, PACK, P])
             for j in range(PACK):
-                nc.tensor.matmul_mx(out=acc[:, j, :], lhsT=val_codes[j][:].bitcast(FP8X4),
-                                    lhsT_scale=val_scales[j][:], rhs=w_mx[h][0][:].bitcast(FP8X4),
-                                    rhs_scale=w_mx[h][1][:], start=True, stop=True)
-            nc.vector.tensor_copy(result_bf[:, half_cols[h], :].rearrange("p (g r) j -> p g r j", r=TEAM),
-                                  acc[:].rearrange("p j (r g) -> p g r j", r=TEAM))
-            nc.scalar.copy(result[h][:].rearrange("p j (g r) -> p j g r", r=TEAM),
+                nc.tensor.matmul_mx(out=acc[:, j, :], lhsT=val_mx[j][0].bitcast(FP8X4),
+                                    lhsT_scale=val_mx[j][1], rhs=w_codes[:].bitcast(FP8X4),
+                                    rhs_scale=w_scales[:], start=True, stop=True)
+            result_bf = sb("result_bf%d" % h, [P, P, PACK], BF16)
+            round_copy(result_bf[:].rearrange("p (g r) j -> p g r j", r=TEAM),
+                       acc[:].rearrange("p j (r g) -> p g r j", r=TEAM))
+            result = sb("result%d" % h, [P, PACK, P], F32)
+            nc.scalar.copy(result[:].rearrange("p j (g r) -> p j g r", r=TEAM),
                            acc[:].rearrange("p j (r g) -> p j g r", r=TEAM))
-            nc.scalar.dma_start(out_rows[:, :, half_cols[h]], result[h][:])
-        nc.vector.quantize_mx(out_codes[:].bitcast(FP8X4), out_scales[:], result_bf[:].rearrange("p q j -> p (q j)"))
+            nc.sync.dma_start(out_rows[:, :, half_cols[h]], result[:])
+            return result_bf
+
+        def planes(h, result_bf):
+            nc.vector.quantize_mx(out_codes[:, half_cols[h]].bitcast(FP8X4), out_scales[:, half_cols[h]],
+                                  result_bf[:].rearrange("p q j -> p (q j)"))
+
+        listed0 = gather_values(0)
+        both0, ta0 = exp_and_change(0)
+        both1, ta1 = exp_and_change(1)
+        sums0 = team_sums(0, both0)
+        turn_values(0, listed0, "turned0")
+        sums1 = team_sums(1, both1)
+        listed = [gather_values(j) for j in range(1, PACK)]
+        turn_values(1, listed[0], "sums_turned1")
+        turn_values(2, listed[1], "turned0")
+        share0 = share_of(0, sums0)
+        weight0, mean0 = weight_and_mean(0, sums0, share0)
+        turn_values(3, listed[2], "sums0")
+        scaled0, centred0 = factors(0, both0, ta0, weight0, mean0)
+        share1 = share_of(1, sums1)
+        w_bf0 = product(0, scaled0, centred0, None)
+        quantize_values("early", range(early), "mean0")
+        weight1, mean1 = weight_and_mean(1, sums1, share1)
+        w0 = quantize("w0", w_bf0)
+        scaled1, centred1 = factors(1, both1, ta1, weight1, mean1)
+        quantize_values("last", [early], "mean1")
+        result_bf0 = read_values(0, w0[0], w0[1], nc.scalar.copy)
+        w_bf1 = product(1, scaled1, centred1, "last_bf")
+        w1 = quantize("w1", w_bf1)
+        planes(0, result_bf0)
+        result_bf1 = read_values(1, w1[0], w1[1], nc.vector.tensor_copy)
+        planes(1, result_bf1)
         nc.sync.dma_start(out_1[0].rearrange("p c r -> p (c r)").bitcast(I32), out_codes[:].bitcast(I32))
         for quad in range(4):
-            nc.sync.dma_start(out_2[0].bitcast(I32)[4 * quad : 4 * quad + 4, :],
-                              out_scales[:].bitcast(I32)[32 * quad : 32 * quad + 4, :])
+            queue = nc.scalar if quad % 2 else nc.sync
+            queue.dma_start(out_2[0].bitcast(I32)[4 * quad : 4 * quad + 4, :],
+                            out_scales[:].bitcast(I32)[32 * quad : 32 * quad + 4, :])

@@ -24,6 +24,7 @@ PACK = 4
 TEAM = Q // G
 HALVES = 2
 HG = G // HALVES
+ON_SCALAR = 3
 
 
 def tile_attend_ttteamshares_pl_kernel(tc, query, dquery, keys_words, keys_scales, reserve, factor, vals, offs,
@@ -58,12 +59,10 @@ def tile_attend_ttteamshares_pl_kernel(tc, query, dquery, keys_words, keys_scale
         val_rows = vals.rearrange("(p j) t -> j p t", j=PACK)
         val_pool = [sb("val_pool%d" % j, [P, T], F32) for j in range(PACK)]
         for j in range(PACK):
-            nc.sync.dma_start(val_pool[j][:], val_rows[j])
+            width = T // 2 if j == ON_SCALAR else T
+            for c0 in range(0, T, width):
+                nc.sync.dma_start(val_pool[j][:, c0 : c0 + width], val_rows[j][:, c0 : c0 + width])
 
-        zeros = sb("zeros", [P, 8], F32)
-        nc.gpsimd.memset(zeros[:], 0.0)
-        warm = sb("warm", [P, 8], F32)
-        nc.scalar.activation(warm[:], zeros[:], EXP)
         identity = sb("identity", [P, P], F32)
         make_identity(nc, identity[:])
         reserve_wide = sb("reserve_wide", [P, 2, HG, PACK], F32)
@@ -79,16 +78,15 @@ def tile_attend_ttteamshares_pl_kernel(tc, query, dquery, keys_words, keys_scale
         nc.vector.tensor_copy(key_scales[:], scale_listed[:].rearrange("p (s t) -> p t s", t=PACK))
         nc.vector.tensor_copy(key_words[:], key_listed[:].rearrange("p (s t) -> p t s", t=PACK))
 
-        def interleave(copy, name, raw, cols):
-            width = cols.stop - cols.start
-            grouped = sb(name, [P, width, PACK], BF16)
-            copy(grouped[:].rearrange("p (c i) j -> p c j i", i=4),
-                 raw[:, :, cols].rearrange("p j (c i) -> p c j i", i=4))
+        def interleave(name, raw):
+            grouped = sb(name, [P, Q, PACK], BF16)
+            nc.scalar.activation(grouped[:].rearrange("p (c i) j -> p c j i", i=4),
+                                 raw[:].rearrange("p j (c i) -> p c j i", i=4), COPY)
             return grouped
 
-        def quantize(name, grouped):
+        def quantize(name, grouped, tag=None):
             width = grouped.shape[1]
-            codes = sb(name + "_codes", [P, width], U32)
+            codes = sb(name + "_codes", [P, width], U32, tag=tag)
             scales = sb(name + "_scales", [P, width], U8)
             nc.vector.quantize_mx(codes[:].bitcast(FP8X4), scales[:], grouped[:].rearrange("p q j -> p (q j)"))
             return codes, scales
@@ -102,19 +100,15 @@ def tile_attend_ttteamshares_pl_kernel(tc, query, dquery, keys_words, keys_scale
             return acc[:].rearrange("p t (g r) -> p r g t", r=TEAM)
 
         half_cols = [slice(P * h, P * (h + 1)) for h in range(HALVES)]
-        q_bf = interleave(nc.scalar.copy, "q_bf", q_raw[0], slice(0, Q))
-        dq_bf = interleave(nc.scalar.copy, "dq_bf", q_raw[1], slice(0, Q))
+        q_bf = interleave("q_bf", q_raw[0])
+        dq_bf = interleave("dq_bf", q_raw[1])
         q_codes, q_scales = quantize("q", q_bf)
         dq_codes, dq_scales = quantize("dq", dq_bf)
 
-        early = PACK - 1
-        early_bf = sb("early_bf", [P, early * P, PACK], BF16)
-        last_bf = sb("last_bf", [P, P, PACK], BF16)
-        val_bf = [early_bf[:, P * j : P * (j + 1), :] for j in range(early)] + [last_bf[:]]
 
         def gather_values(j):
             listed = sb("val_listed%d" % j, [P, I], BF16)
-            if j < early:
+            if j != ON_SCALAR:
                 nc.vector.tensor_copy(listed[:], val_pool[j][:].indirect(offsets[:]))
             else:
                 rounded = sb("val_rounded", [P, T], BF16)
@@ -123,28 +117,19 @@ def tile_attend_ttteamshares_pl_kernel(tc, query, dquery, keys_words, keys_scale
                 nc.scalar.activation(listed[:], rounded[:].indirect(offsets[:]), COPY)
             return listed
 
-        def turn_values(j, listed, tag):
-            pairs = listed[:].bitcast(F32)
-            turned = bank("turned%d" % j, tag, [P, 2, P])
-            for u in range(2):
-                nc.tensor.transpose(turned[:, u, :], pairs[:, u : 2 * P : 2], identity[:])
-            nc.scalar.copy(val_bf[j].bitcast(F32), turned[:].rearrange("p u e -> p e u"))
-
-        val_mx = {}
-
-        def quantize_values(name, planes_in, tag):
-            codes = sb(name + "_codes", [P, len(planes_in) * P], U32, tag=tag)
-            scales = sb(name + "_scales", [P, len(planes_in) * P], U8)
-            for n, j in enumerate(planes_in):
-                cols = slice(P * n, P * (n + 1))
-                nc.vector.quantize_mx(codes[:, cols].bitcast(FP8X4), scales[:, cols],
-                                      val_bf[j].rearrange("p e t -> p (e t)"))
-                val_mx[j] = (codes[:, cols], scales[:, cols])
+        def turn_values(first, listed, tag):
+            turned = bank("turned%d" % first, tag, [P, 2, 2, P])
+            for n in range(2):
+                pairs = listed[first + n][:].bitcast(F32)
+                for u in range(2):
+                    nc.tensor.transpose(turned[:, n, u, :], pairs[:, u : 2 * P : 2], identity[:])
+            nc.scalar.copy(val_bf[:, P * first : P * (first + 2), :].bitcast(F32).rearrange("p (n e) u -> p n e u", n=2),
+                           turned[:].rearrange("p n u e -> p n e u"))
 
         def exp_and_change(h):
             a_bank = scores("score%d" % h, "score%d" % h, q_codes[:, half_cols[h]], q_scales[:, half_cols[h]])
             ta_bank = scores("tangent%d" % h, "tangent%d" % h, dq_codes[:, half_cols[h]], dq_scales[:, half_cols[h]])
-            both = sb("both%d" % h, [P, TEAM, 2, HG, PACK], F32, tag="val_pool0" if h == 0 else None)
+            both = both_halves[:, h]
             nc.scalar.activation(both[:, :, 0], a_bank, EXP)
             nc.vector.tensor_tensor(both[:, :, 1], ta_bank, both[:, :, 0], MULT)
             return both, ta_bank
@@ -166,7 +151,7 @@ def tile_attend_ttteamshares_pl_kernel(tc, query, dquery, keys_words, keys_scale
         row_shape = [P, TEAM, HG, PACK]
 
         def share_of(h, sums):
-            share = sb("share%d" % h, team_shape, F32, tag=("val_pool2", "weight0")[h])
+            share = sb("share%d" % h, team_shape, F32, tag="val_pool2")
             nc.vector.reciprocal(share[:], sums[:, 0])
             return share
 
@@ -179,9 +164,14 @@ def tile_attend_ttteamshares_pl_kernel(tc, query, dquery, keys_words, keys_scale
 
         def factors(h, both, ta_bank, weight, mean):
             scaled = sb("scaled%d" % h, row_shape, F32)
-            nc.vector.tensor_tensor(scaled[:], both[:, :, 0], weight[:].unsqueeze(1).to_broadcast(row_shape), MULT)
+            rows = (TEAM, TEAM // 2)[h]
+            nc.gpsimd.tensor_tensor(scaled[:, :rows], both[:, :rows, 0],
+                                    weight[:].unsqueeze(1).to_broadcast([P, rows, HG, PACK]), MULT)
             centred = sb("centred%d" % h, row_shape, F32)
             nc.vector.tensor_tensor(centred[:], ta_bank, mean[:].unsqueeze(1).to_broadcast(row_shape), SUB)
+            if rows < TEAM:
+                nc.vector.tensor_tensor(scaled[:, rows:], both[:, rows:, 0],
+                                        weight[:].unsqueeze(1).to_broadcast([P, TEAM - rows, HG, PACK]), MULT)
             return scaled, centred
 
         def product(h, scaled, centred, tag):
@@ -192,13 +182,14 @@ def tile_attend_ttteamshares_pl_kernel(tc, query, dquery, keys_words, keys_scale
 
         out_codes = sb("out_codes", [P, Q], U32)
         out_scales = sb("out_scales", [P, Q], U8)
+        out_words = out_1[0].rearrange("p c r -> p (c r)").bitcast(I32)
         out_rows = out_0.rearrange("(p j) q -> p j q", j=PACK)
 
         def read_values(h, w_codes, w_scales, round_copy):
             acc = bank("out%d" % h, "score%d" % h, [P, PACK, P])
             for j in range(PACK):
-                nc.tensor.matmul_mx(out=acc[:, j, :], lhsT=val_mx[j][0].bitcast(FP8X4),
-                                    lhsT_scale=val_mx[j][1], rhs=w_codes[:].bitcast(FP8X4),
+                nc.tensor.matmul_mx(out=acc[:, j, :], lhsT=val_codes[:, P * j : P * (j + 1)].bitcast(FP8X4),
+                                    lhsT_scale=val_scales[:, P * j : P * (j + 1)], rhs=w_codes[:].bitcast(FP8X4),
                                     rhs_scale=w_scales[:], start=True, stop=True)
             result_bf = sb("result_bf%d" % h, [P, P, PACK], BF16)
             round_copy(result_bf[:].rearrange("p (g r) j -> p g r j", r=TEAM),
@@ -212,34 +203,33 @@ def tile_attend_ttteamshares_pl_kernel(tc, query, dquery, keys_words, keys_scale
         def planes(h, result_bf):
             nc.vector.quantize_mx(out_codes[:, half_cols[h]].bitcast(FP8X4), out_scales[:, half_cols[h]],
                                   result_bf[:].rearrange("p q j -> p (q j)"))
+            nc.sync.dma_start(out_words[:, half_cols[h]], out_codes[:, half_cols[h]].bitcast(I32))
 
         listed0 = gather_values(0)
+        both_halves = sb("both_halves", [P, HALVES, TEAM, 2, HG, PACK], F32, tag="val_pool0")
         both0, ta0 = exp_and_change(0)
         both1, ta1 = exp_and_change(1)
         sums0 = team_sums(0, both0)
-        turn_values(0, listed0, "turned0")
         sums1 = team_sums(1, both1)
-        listed = [gather_values(j) for j in range(1, PACK)]
-        turn_values(1, listed[0], "sums_turned1")
-        turn_values(2, listed[1], "turned0")
+        listed = [listed0] + [gather_values(j) for j in range(1, PACK)]
+        val_bf = sb("val_bf", [P, E, PACK], BF16, tag="val_rounded")
+        turn_values(0, listed, "turned0")
+        turn_values(2, listed, "sums_turned1")
         share0 = share_of(0, sums0)
         weight0, mean0 = weight_and_mean(0, sums0, share0)
-        turn_values(3, listed[2], "sums0")
         scaled0, centred0 = factors(0, both0, ta0, weight0, mean0)
         share1 = share_of(1, sums1)
         w_bf0 = product(0, scaled0, centred0, None)
-        quantize_values("early", range(early), "mean0")
-        weight1, mean1 = weight_and_mean(1, sums1, share1)
         w0 = quantize("w0", w_bf0)
+        weight1, mean1 = weight_and_mean(1, sums1, share1)
         scaled1, centred1 = factors(1, both1, ta1, weight1, mean1)
-        quantize_values("last", [early], "mean1")
+        val_codes, val_scales = quantize("val", val_bf, "mean1")
         result_bf0 = read_values(0, w0[0], w0[1], nc.scalar.copy)
-        w_bf1 = product(1, scaled1, centred1, "last_bf")
+        w_bf1 = product(1, scaled1, centred1, "val_rounded")
         w1 = quantize("w1", w_bf1)
         planes(0, result_bf0)
         result_bf1 = read_values(1, w1[0], w1[1], nc.vector.tensor_copy)
         planes(1, result_bf1)
-        nc.sync.dma_start(out_1[0].rearrange("p c r -> p (c r)").bitcast(I32), out_codes[:].bitcast(I32))
         for quad in range(4):
             queue = nc.scalar if quad % 2 else nc.sync
             queue.dma_start(out_2[0].bitcast(I32)[4 * quad : 4 * quad + 4, :],

@@ -24,7 +24,7 @@ PACK = 4
 TEAM = Q // G
 HALVES = 2
 HG = G // HALVES
-ON_SCALAR = 3
+ON_SCALAR = 2
 
 
 def tile_attend_ttteamshares_pl_kernel(tc, query, dquery, keys_words, keys_scales, reserve, factor, vals, offs,
@@ -45,10 +45,10 @@ def tile_attend_ttteamshares_pl_kernel(tc, query, dquery, keys_words, keys_scale
         key_scale_pool = sb("key_scale_pool", [P, T], U8)
         nc.gpsimd.memset(key_scale_pool[:].bitcast(I32), 0)
         nc.sync.dma_start(offsets[:], offs)
+        nc.sync.dma_start(key_pool[:].bitcast(I32), keys_words[0].bitcast(I32))
         for quad in range(4):
             nc.sync.dma_start(key_scale_pool[:].bitcast(I32)[32 * quad : 32 * quad + 4, :],
                               keys_scales[0].bitcast(I32)[4 * quad : 4 * quad + 4, :])
-        nc.sync.dma_start(key_pool[:].bitcast(I32), keys_words[0].bitcast(I32))
         q_raw = [sb("q_raw%d" % n, [P, PACK, Q], F32) for n in range(2)]
         for n, src in enumerate((query, dquery)):
             nc.sync.dma_start(q_raw[n][:], src.rearrange("(p j) q -> p j q", j=PACK))
@@ -57,11 +57,13 @@ def tile_attend_ttteamshares_pl_kernel(tc, query, dquery, keys_words, keys_scale
         nc.sync.dma_start(slot_reserve[:], reserve.rearrange("(p t) o -> p (t o)", t=PACK))
         nc.sync.dma_start(slot_factor[:], factor.rearrange("(p t) o -> p (t o)", t=PACK))
         val_rows = vals.rearrange("(p j) t -> j p t", j=PACK)
-        val_pool = [sb("val_pool%d" % j, [P, T], F32) for j in range(PACK)]
+        val_pool = []
         for j in range(PACK):
             width = T // 2 if j == ON_SCALAR else T
-            for c0 in range(0, T, width):
-                nc.sync.dma_start(val_pool[j][:, c0 : c0 + width], val_rows[j][:, c0 : c0 + width])
+            parts = [sb("val_pool%d_%d" % (j, n), [P, width], F32) for n in range(T // width)]
+            for n, part in enumerate(parts):
+                nc.sync.dma_start(part[:], val_rows[j][:, width * n : width * (n + 1)])
+            val_pool.append(parts)
 
         identity = sb("identity", [P, P], F32)
         make_identity(nc, identity[:])
@@ -73,10 +75,10 @@ def tile_attend_ttteamshares_pl_kernel(tc, query, dquery, keys_words, keys_scale
         key_words = sb("key_words", [P, PACK, P], U16)
         scale_listed = sb("scale_listed", [P, I], U8)
         key_scales = sb("key_scales", [P, PACK, P], U8)
-        nc.vector.tensor_copy(scale_listed[:], key_scale_pool[:].indirect(offsets[:]))
         nc.vector.tensor_copy(key_listed[:], key_pool[:].indirect(offsets[:]))
-        nc.vector.tensor_copy(key_scales[:], scale_listed[:].rearrange("p (s t) -> p t s", t=PACK))
+        nc.vector.tensor_copy(scale_listed[:], key_scale_pool[:].indirect(offsets[:]))
         nc.vector.tensor_copy(key_words[:], key_listed[:].rearrange("p (s t) -> p t s", t=PACK))
+        nc.vector.tensor_copy(key_scales[:], scale_listed[:].rearrange("p (s t) -> p t s", t=PACK))
 
         def interleave(name, raw):
             grouped = sb(name, [P, Q, PACK], BF16)
@@ -109,22 +111,25 @@ def tile_attend_ttteamshares_pl_kernel(tc, query, dquery, keys_words, keys_scale
         def gather_values(j):
             listed = sb("val_listed%d" % j, [P, I], BF16)
             if j != ON_SCALAR:
-                nc.vector.tensor_copy(listed[:], val_pool[j][:].indirect(offsets[:]))
+                nc.vector.tensor_copy(listed[:], val_pool[j][0][:].indirect(offsets[:]))
             else:
                 rounded = sb("val_rounded", [P, T], BF16)
                 for c0 in range(0, T, I):
-                    nc.scalar.activation(rounded[:, c0 : c0 + I], val_pool[j][:, c0 : c0 + I], COPY)
+                    n, start = divmod(c0, T // 2)
+                    nc.scalar.activation(rounded[:, c0 : c0 + I], val_pool[j][n][:, start : start + I], COPY)
                 nc.scalar.activation(listed[:], rounded[:].indirect(offsets[:]), COPY)
             return listed
 
-        def turn_values(first, listed, tag):
+        def turn_values(first, listed, tag, sb_tag):
             turned = bank("turned%d" % first, tag, [P, 2, 2, P])
             for n in range(2):
                 pairs = listed[first + n][:].bitcast(F32)
                 for u in range(2):
                     nc.tensor.transpose(turned[:, n, u, :], pairs[:, u : 2 * P : 2], identity[:])
-            nc.scalar.copy(val_bf[:, P * first : P * (first + 2), :].bitcast(F32).rearrange("p (n e) u -> p n e u", n=2),
+            val_bf = sb("val_bf%d" % first, [P, 2 * P, PACK], BF16, tag=sb_tag)
+            nc.scalar.copy(val_bf[:].bitcast(F32).rearrange("p (n e) u -> p n e u", n=2),
                            turned[:].rearrange("p n u e -> p n e u"))
+            return val_bf
 
         def exp_and_change(h):
             a_bank = scores("score%d" % h, "score%d" % h, q_codes[:, half_cols[h]], q_scales[:, half_cols[h]])
@@ -135,13 +140,13 @@ def tile_attend_ttteamshares_pl_kernel(tc, query, dquery, keys_words, keys_scale
             return both, ta_bank
 
         def team_sums(h, both):
-            slabs = [both[:, r].rearrange("p k g t -> p (k g t)") for r in range(TEAM)]
-            slabs.append(reserve_wide[:].rearrange("p k g t -> p (k g t)"))
+            slabs = [reserve_wide[:].rearrange("p k g t -> p (k g t)")]
+            slabs.extend(both[:, r].rearrange("p k g t -> p (k g t)") for r in range(TEAM))
             turned = bank("sums_turned%d" % h, "sums_turned%d" % h, [P, P])
             for n, slab in enumerate(slabs):
                 nc.tensor.matmul(turned[:], lhsT=slab, rhs=identity[:], is_transpose=True,
                                  start=(n == 0), stop=(n == len(slabs) - 1))
-            turned_sb = sb("sums_turned_sb%d" % h, [P, P], F32)
+            turned_sb = sb("sums_turned_sb%d" % h, [P, P], F32, tag=(None, "val_pool2_0")[h])
             nc.scalar.copy(turned_sb[:], turned[:])
             sums = bank("sums%d" % h, ("sums0", "sums_turned0")[h], [P, 2, HG, PACK])
             nc.tensor.transpose(sums[:].rearrange("p k g t -> p (k g t)"), turned_sb[:], identity[:])
@@ -151,7 +156,7 @@ def tile_attend_ttteamshares_pl_kernel(tc, query, dquery, keys_words, keys_scale
         row_shape = [P, TEAM, HG, PACK]
 
         def share_of(h, sums):
-            share = sb("share%d" % h, team_shape, F32, tag="val_pool2")
+            share = sb("share%d" % h, team_shape, F32, tag="val_pool1_0")
             nc.vector.reciprocal(share[:], sums[:, 0])
             return share
 
@@ -164,14 +169,9 @@ def tile_attend_ttteamshares_pl_kernel(tc, query, dquery, keys_words, keys_scale
 
         def factors(h, both, ta_bank, weight, mean):
             scaled = sb("scaled%d" % h, row_shape, F32)
-            rows = (TEAM, TEAM // 2)[h]
-            nc.gpsimd.tensor_tensor(scaled[:, :rows], both[:, :rows, 0],
-                                    weight[:].unsqueeze(1).to_broadcast([P, rows, HG, PACK]), MULT)
+            nc.gpsimd.tensor_tensor(scaled[:], both[:, :, 0], weight[:].unsqueeze(1).to_broadcast(row_shape), MULT)
             centred = sb("centred%d" % h, row_shape, F32)
             nc.vector.tensor_tensor(centred[:], ta_bank, mean[:].unsqueeze(1).to_broadcast(row_shape), SUB)
-            if rows < TEAM:
-                nc.vector.tensor_tensor(scaled[:, rows:], both[:, rows:, 0],
-                                        weight[:].unsqueeze(1).to_broadcast([P, TEAM - rows, HG, PACK]), MULT)
             return scaled, centred
 
         def product(h, scaled, centred, tag):
@@ -185,20 +185,28 @@ def tile_attend_ttteamshares_pl_kernel(tc, query, dquery, keys_words, keys_scale
         out_words = out_1[0].rearrange("p c r -> p (c r)").bitcast(I32)
         out_rows = out_0.rearrange("(p j) q -> p j q", j=PACK)
 
-        def read_values(h, w_codes, w_scales, round_copy):
+        def read_values(h, w_codes, w_scales):
             acc = bank("out%d" % h, "score%d" % h, [P, PACK, P])
             for j in range(PACK):
-                nc.tensor.matmul_mx(out=acc[:, j, :], lhsT=val_codes[:, P * j : P * (j + 1)].bitcast(FP8X4),
-                                    lhsT_scale=val_scales[:, P * j : P * (j + 1)], rhs=w_codes[:].bitcast(FP8X4),
+                val_codes, val_scales = val_mx[j // 2]
+                cols = half_cols[j % 2]
+                nc.tensor.matmul_mx(out=acc[:, j, :], lhsT=val_codes[:, cols].bitcast(FP8X4),
+                                    lhsT_scale=val_scales[:, cols], rhs=w_codes[:].bitcast(FP8X4),
                                     rhs_scale=w_scales[:], start=True, stop=True)
+            return acc
+
+        def round_result(h, acc):
             result_bf = sb("result_bf%d" % h, [P, P, PACK], BF16)
-            round_copy(result_bf[:].rearrange("p (g r) j -> p g r j", r=TEAM),
-                       acc[:].rearrange("p j (r g) -> p g r j", r=TEAM))
+            nc.vector.tensor_copy(result_bf[:].rearrange("p (g r) j -> p g r j", r=TEAM),
+                                  acc[:].rearrange("p j (r g) -> p g r j", r=TEAM))
+            return result_bf
+
+        def store_result(h, acc):
             result = sb("result%d" % h, [P, PACK, P], F32)
             nc.scalar.copy(result[:].rearrange("p j (g r) -> p j g r", r=TEAM),
                            acc[:].rearrange("p j (r g) -> p j g r", r=TEAM))
             nc.sync.dma_start(out_rows[:, :, half_cols[h]], result[:])
-            return result_bf
+            return result
 
         def planes(h, result_bf):
             nc.vector.quantize_mx(out_codes[:, half_cols[h]].bitcast(FP8X4), out_scales[:, half_cols[h]],
@@ -206,29 +214,34 @@ def tile_attend_ttteamshares_pl_kernel(tc, query, dquery, keys_words, keys_scale
             nc.sync.dma_start(out_words[:, half_cols[h]], out_codes[:, half_cols[h]].bitcast(I32))
 
         listed0 = gather_values(0)
-        both_halves = sb("both_halves", [P, HALVES, TEAM, 2, HG, PACK], F32, tag="val_pool0")
+        both_halves = sb("both_halves", [P, HALVES, TEAM, 2, HG, PACK], F32, tag="val_pool0_0")
         both0, ta0 = exp_and_change(0)
         both1, ta1 = exp_and_change(1)
         sums0 = team_sums(0, both0)
-        sums1 = team_sums(1, both1)
         listed = [listed0] + [gather_values(j) for j in range(1, PACK)]
-        val_bf = sb("val_bf", [P, E, PACK], BF16, tag="val_rounded")
-        turn_values(0, listed, "turned0")
-        turn_values(2, listed, "sums_turned1")
+        sums1 = team_sums(1, both1)
+        val_bf = [turn_values(0, listed, "turned0", "val_rounded"), turn_values(2, listed, "sums_turned1", None)]
         share0 = share_of(0, sums0)
         weight0, mean0 = weight_and_mean(0, sums0, share0)
         scaled0, centred0 = factors(0, both0, ta0, weight0, mean0)
         share1 = share_of(1, sums1)
-        w_bf0 = product(0, scaled0, centred0, None)
-        w0 = quantize("w0", w_bf0)
         weight1, mean1 = weight_and_mean(1, sums1, share1)
         scaled1, centred1 = factors(1, both1, ta1, weight1, mean1)
-        val_codes, val_scales = quantize("val", val_bf, "mean1")
-        result_bf0 = read_values(0, w0[0], w0[1], nc.scalar.copy)
-        w_bf1 = product(1, scaled1, centred1, "val_rounded")
+        w_bf0 = product(0, scaled0, centred0, "val_pool3_0")
+        val_mx = [quantize("val0", val_bf[0], "mean1")]
+        w0 = quantize("w0", w_bf0)
+        w_bf1 = product(1, scaled1, centred1, "centred0")
+        val_mx.append(quantize("val2", val_bf[1]))
         w1 = quantize("w1", w_bf1)
+        acc0 = read_values(0, w0[0], w0[1])
+        acc1 = read_values(1, w1[0], w1[1])
+        result_bf0 = round_result(0, acc0)
+        result1 = store_result(1, acc1)
         planes(0, result_bf0)
-        result_bf1 = read_values(1, w1[0], w1[1], nc.vector.tensor_copy)
+        result_bf1 = sb("result_bf1", [P, P, PACK], BF16)
+        nc.vector.tensor_copy(result_bf1[:].rearrange("p (c i) j -> p c j i", i=4),
+                              result1[:].rearrange("p j (c i) -> p c j i", i=4))
+        store_result(0, acc0)
         planes(1, result_bf1)
         for quad in range(4):
             queue = nc.scalar if quad % 2 else nc.sync

@@ -4,7 +4,7 @@ import concourse.mybir as mybir
 from concourse.masks import make_identity
 
 D, E, T, I, Q, G = 512, 512, 2048, 512, 256, 32
-FLOPS = 2 * D * I * Q * 2 + 2 * I * E * Q
+FLOPS = 2 * (2 * D * I * Q) + 2 * I * E * Q
 
 F32 = mybir.dt.float32
 BF16 = mybir.dt.bfloat16
@@ -22,8 +22,12 @@ EXP = mybir.ActivationFunctionType.Exp
 P = 128
 PACK = 4
 TEAM = Q // G
-HALVES = 2
+HALVES = Q // P
 HG = G // HALVES
+QUADS, QUAD = 4, 32
+ROWS = 4
+LIST_GROUP = 16
+RUN = 4
 ON_SCALAR = 2
 
 
@@ -34,24 +38,24 @@ def tile_attend_ttteamshares_pl_kernel(tc, query, dquery, keys_words, keys_scale
         held = ctx.enter_context(tc.tile_pool(name="held", bufs=1))
         psum = ctx.enter_context(tc.psum_pool(name="psum", bufs=1))
 
-        def sb(name, shape, dtype, tag=None):
-            return held.tile(shape, dtype, name=name, tag=tag or name, align_bytes=64)
+        def sb(name, shape, dtype, reuse=None):
+            return held.tile(shape, dtype, name=name, tag=reuse or name, align_bytes=64)
 
-        def bank(name, tag, shape):
-            return psum.tile(shape, F32, name=name, tag=tag)
+        def bank(name, shape, reuse=None):
+            return psum.tile(shape, F32, name=name, tag=reuse or name)
 
-        offsets = held.tile([P, I // 16], U16, name="offsets")
+        offsets = held.tile([P, I // LIST_GROUP], U16, name="offsets")
         key_pool = sb("key_pool", [P, T], U16)
         key_scale_pool = sb("key_scale_pool", [P, T], U8)
         nc.gpsimd.memset(key_scale_pool[:].bitcast(I32), 0)
         nc.sync.dma_start(offsets[:], offs)
         nc.sync.dma_start(key_pool[:].bitcast(I32), keys_words[0].bitcast(I32))
-        for quad in range(4):
-            nc.sync.dma_start(key_scale_pool[:].bitcast(I32)[32 * quad : 32 * quad + 4, :],
-                              keys_scales[0].bitcast(I32)[4 * quad : 4 * quad + 4, :])
+        for quad in range(QUADS):
+            nc.sync.dma_start(key_scale_pool[:].bitcast(I32)[QUAD * quad : QUAD * quad + ROWS, :],
+                              keys_scales[0].bitcast(I32)[ROWS * quad : ROWS * (quad + 1), :])
         q_raw = [sb("q_raw%d" % n, [P, PACK, Q], F32) for n in range(2)]
         for n, src in enumerate((query, dquery)):
-            nc.sync.dma_start(q_raw[n][:], src.rearrange("(p j) q -> p j q", j=PACK))
+            nc.sync.dma_start(q_raw[n][:], src.rearrange("(p t) q -> p t q", t=PACK))
         slot_reserve = sb("slot_reserve", [P, PACK], F32)
         slot_factor = sb("slot_factor", [P, PACK], F32)
         nc.sync.dma_start(slot_reserve[:], reserve.rearrange("(p t) o -> p (t o)", t=PACK))
@@ -67,9 +71,8 @@ def tile_attend_ttteamshares_pl_kernel(tc, query, dquery, keys_words, keys_scale
 
         identity = sb("identity", [P, P], F32)
         make_identity(nc, identity[:])
-        reserve_wide = sb("reserve_wide", [P, 2, HG, PACK], F32)
-        nc.gpsimd.memset(reserve_wide[:, 1], 0.0)
-        nc.gpsimd.tensor_copy(reserve_wide[:, 0], slot_reserve[:].unsqueeze(1).to_broadcast([P, HG, PACK]))
+        reserve_wide = sb("reserve_wide", [P, G, PACK], F32)
+        nc.gpsimd.tensor_copy(reserve_wide[:], slot_reserve[:].unsqueeze(1).to_broadcast([P, G, PACK]))
 
         key_listed = sb("key_listed", [P, I], U16)
         key_words = sb("key_words", [P, PACK, P], U16)
@@ -80,33 +83,37 @@ def tile_attend_ttteamshares_pl_kernel(tc, query, dquery, keys_words, keys_scale
         nc.vector.tensor_copy(key_words[:], key_listed[:].rearrange("p (s t) -> p t s", t=PACK))
         nc.vector.tensor_copy(key_scales[:], scale_listed[:].rearrange("p (s t) -> p t s", t=PACK))
 
-        def interleave(name, raw):
+        def interleaved(grouped, rows):
+            return (grouped[:].rearrange("p (c i) t -> p c t i", i=RUN),
+                    rows[:].rearrange("p t (c i) -> p c t i", i=RUN))
+
+        def round_queries(name, raw):
             grouped = sb(name, [P, Q, PACK], BF16)
-            nc.scalar.activation(grouped[:].rearrange("p (c i) j -> p c j i", i=4),
-                                 raw[:].rearrange("p j (c i) -> p c j i", i=4), COPY)
+            nc.scalar.activation(*interleaved(grouped, raw), COPY)
             return grouped
 
-        def quantize(name, grouped, tag=None):
+        def quantize(name, grouped, reuse=None):
             width = grouped.shape[1]
-            codes = sb(name + "_codes", [P, width], U32, tag=tag)
+            codes = sb(name + "_codes", [P, width], U32, reuse=reuse)
             scales = sb(name + "_scales", [P, width], U8)
-            nc.vector.quantize_mx(codes[:].bitcast(FP8X4), scales[:], grouped[:].rearrange("p q j -> p (q j)"))
+            nc.vector.quantize_mx(codes[:].bitcast(FP8X4), scales[:], grouped[:].rearrange("p c t -> p (c t)"))
             return codes, scales
 
-        def scores(name, tag, codes, scales):
-            acc = bank(name, tag, [P, PACK, P])
+        def scores(name, codes, scales):
+            acc = bank(name, [P, PACK, P])
             for t in range(PACK):
                 nc.tensor.matmul_mx(out=acc[:, t, :], lhsT=key_words[:, t, :].bitcast(FP4X4),
                                     lhsT_scale=key_scales[:, t, :], rhs=codes.bitcast(FP8X4),
                                     rhs_scale=scales, start=True, stop=True)
             return acc[:].rearrange("p t (g r) -> p r g t", r=TEAM)
 
-        half_cols = [slice(P * h, P * (h + 1)) for h in range(HALVES)]
-        q_bf = interleave("q_bf", q_raw[0])
-        dq_bf = interleave("dq_bf", q_raw[1])
+        def block(n):
+            return slice(P * n, P * (n + 1))
+
+        q_bf = round_queries("q_bf", q_raw[0])
+        dq_bf = round_queries("dq_bf", q_raw[1])
         q_codes, q_scales = quantize("q", q_bf)
         dq_codes, dq_scales = quantize("dq", dq_bf)
-
 
         def gather_values(j):
             listed = sb("val_listed%d" % j, [P, I], BF16)
@@ -120,65 +127,39 @@ def tile_attend_ttteamshares_pl_kernel(tc, query, dquery, keys_words, keys_scale
                 nc.scalar.activation(listed[:], rounded[:].indirect(offsets[:]), COPY)
             return listed
 
-        def turn_values(first, listed, tag, sb_tag):
-            turned = bank("turned%d" % first, tag, [P, 2, 2, P])
+        def turn_values(first, listed, bank_reuse, sb_reuse):
+            turned = bank("turned%d" % first, [P, 2, 2, P], reuse=bank_reuse)
             for n in range(2):
                 pairs = listed[first + n][:].bitcast(F32)
                 for u in range(2):
                     nc.tensor.transpose(turned[:, n, u, :], pairs[:, u : 2 * P : 2], identity[:])
-            val_bf = sb("val_bf%d" % first, [P, 2 * P, PACK], BF16, tag=sb_tag)
-            nc.scalar.copy(val_bf[:].bitcast(F32).rearrange("p (n e) u -> p n e u", n=2),
+            grouped = sb("val_bf%d" % first, [P, 2 * P, PACK], BF16, reuse=sb_reuse)
+            nc.scalar.copy(grouped[:].bitcast(F32).rearrange("p (n e) u -> p n e u", n=2),
                            turned[:].rearrange("p n u e -> p n e u"))
-            return val_bf
+            return grouped
 
-        def exp_and_change(h):
-            a_bank = scores("score%d" % h, "score%d" % h, q_codes[:, half_cols[h]], q_scales[:, half_cols[h]])
-            ta_bank = scores("tangent%d" % h, "tangent%d" % h, dq_codes[:, half_cols[h]], dq_scales[:, half_cols[h]])
-            both = both_halves[:, h]
-            nc.scalar.activation(both[:, :, 0], a_bank, EXP)
-            nc.vector.tensor_tensor(both[:, :, 1], ta_bank, both[:, :, 0], MULT)
-            return both, ta_bank
-
-        def team_sums(h, both):
-            slabs = [reserve_wide[:].rearrange("p k g t -> p (k g t)")]
-            slabs.extend(both[:, r].rearrange("p k g t -> p (k g t)") for r in range(TEAM))
-            turned = bank("sums_turned%d" % h, "sums_turned%d" % h, [P, P])
-            for n, slab in enumerate(slabs):
-                nc.tensor.matmul(turned[:], lhsT=slab, rhs=identity[:], is_transpose=True,
-                                 start=(n == 0), stop=(n == len(slabs) - 1))
-            turned_sb = sb("sums_turned_sb%d" % h, [P, P], F32, tag=(None, "val_pool2_0")[h])
+        def team_sums(name, first_terms, rows, sb_reuse):
+            terms = first_terms + [rows[:, r].rearrange("p h g t -> p (h g t)") for r in range(TEAM)]
+            turned = bank(name + "_turned", [P, P])
+            for n, term in enumerate(terms):
+                nc.tensor.matmul(turned[:], lhsT=term, rhs=identity[:], is_transpose=True,
+                                 start=(n == 0), stop=(n == len(terms) - 1))
+            turned_sb = sb(name + "_turned_sb", [P, P], F32, reuse=sb_reuse)
             nc.scalar.copy(turned_sb[:], turned[:])
-            sums = bank("sums%d" % h, ("sums0", "sums_turned0")[h], [P, 2, HG, PACK])
-            nc.tensor.transpose(sums[:].rearrange("p k g t -> p (k g t)"), turned_sb[:], identity[:])
+            sums = bank(name, [P, P])
+            nc.tensor.transpose(sums[:], turned_sb[:], identity[:])
             return sums
 
-        team_shape = [P, HG, PACK]
-        row_shape = [P, TEAM, HG, PACK]
+        team_shape = [P, HALVES, HG, PACK]
+        half_shape = [P, TEAM, HG, PACK]
+        full_shape = [P, TEAM, HALVES, HG, PACK]
 
-        def share_of(h, sums):
-            share = sb("share%d" % h, team_shape, F32, tag="val_pool1_0")
-            nc.vector.reciprocal(share[:], sums[:, 0])
-            return share
-
-        def weight_and_mean(h, sums, share):
-            weight = sb("weight%d" % h, team_shape, F32)
-            nc.vector.tensor_tensor(weight[:], share[:], slot_factor[:].unsqueeze(1).to_broadcast(team_shape), MULT)
-            mean = sb("mean%d" % h, team_shape, F32)
-            nc.vector.tensor_tensor(mean[:], sums[:, 1], share[:], MULT)
-            return weight, mean
-
-        def factors(h, both, ta_bank, weight, mean):
-            scaled = sb("scaled%d" % h, row_shape, F32)
-            nc.gpsimd.tensor_tensor(scaled[:], both[:, :, 0], weight[:].unsqueeze(1).to_broadcast(row_shape), MULT)
-            centred = sb("centred%d" % h, row_shape, F32)
-            nc.vector.tensor_tensor(centred[:], ta_bank, mean[:].unsqueeze(1).to_broadcast(row_shape), SUB)
-            return scaled, centred
-
-        def product(h, scaled, centred, tag):
-            w_bf = sb("w_bf%d" % h, [P, TEAM * HG, PACK], BF16, tag=tag)
-            nc.vector.tensor_tensor(w_bf[:].rearrange("p n t -> p (n t)"), centred[:].rearrange("p r g t -> p (r g t)"),
+        def round_weights(h, scaled, centred, reuse):
+            grouped = sb("w_bf%d" % h, [P, TEAM * HG, PACK], BF16, reuse=reuse)
+            nc.vector.tensor_tensor(grouped[:].rearrange("p n t -> p (n t)"),
+                                    centred[:].rearrange("p r g t -> p (r g t)"),
                                     scaled[:].rearrange("p r g t -> p (r g t)"), MULT)
-            return w_bf
+            return grouped
 
         out_codes = sb("out_codes", [P, Q], U32)
         out_scales = sb("out_scales", [P, Q], U8)
@@ -186,64 +167,74 @@ def tile_attend_ttteamshares_pl_kernel(tc, query, dquery, keys_words, keys_scale
         out_rows = out_0.rearrange("(p j) q -> p j q", j=PACK)
 
         def read_values(h, w_codes, w_scales):
-            acc = bank("out%d" % h, "score%d" % h, [P, PACK, P])
+            acc = bank("out%d" % h, [P, PACK, P], reuse="score%d" % h)
             for j in range(PACK):
                 val_codes, val_scales = val_mx[j // 2]
-                cols = half_cols[j % 2]
-                nc.tensor.matmul_mx(out=acc[:, j, :], lhsT=val_codes[:, cols].bitcast(FP8X4),
-                                    lhsT_scale=val_scales[:, cols], rhs=w_codes[:].bitcast(FP8X4),
+                nc.tensor.matmul_mx(out=acc[:, j, :], lhsT=val_codes[:, block(j % 2)].bitcast(FP8X4),
+                                    lhsT_scale=val_scales[:, block(j % 2)], rhs=w_codes[:].bitcast(FP8X4),
                                     rhs_scale=w_scales[:], start=True, stop=True)
             return acc
-
-        def round_result(h, acc):
-            result_bf = sb("result_bf%d" % h, [P, P, PACK], BF16)
-            nc.vector.tensor_copy(result_bf[:].rearrange("p (g r) j -> p g r j", r=TEAM),
-                                  acc[:].rearrange("p j (r g) -> p g r j", r=TEAM))
-            return result_bf
 
         def store_result(h, acc):
             result = sb("result%d" % h, [P, PACK, P], F32)
             nc.scalar.copy(result[:].rearrange("p j (g r) -> p j g r", r=TEAM),
                            acc[:].rearrange("p j (r g) -> p j g r", r=TEAM))
-            nc.sync.dma_start(out_rows[:, :, half_cols[h]], result[:])
+            nc.sync.dma_start(out_rows[:, :, block(h)], result[:])
             return result
 
-        def planes(h, result_bf):
-            nc.vector.quantize_mx(out_codes[:, half_cols[h]].bitcast(FP8X4), out_scales[:, half_cols[h]],
+        def store_words(h, result_bf):
+            nc.vector.quantize_mx(out_codes[:, block(h)].bitcast(FP8X4), out_scales[:, block(h)],
                                   result_bf[:].rearrange("p q j -> p (q j)"))
-            nc.sync.dma_start(out_words[:, half_cols[h]], out_codes[:, half_cols[h]].bitcast(I32))
+            nc.sync.dma_start(out_words[:, block(h)], out_codes[:, block(h)].bitcast(I32))
 
-        listed0 = gather_values(0)
-        both_halves = sb("both_halves", [P, HALVES, TEAM, 2, HG, PACK], F32, tag="val_pool0_0")
-        both0, ta0 = exp_and_change(0)
-        both1, ta1 = exp_and_change(1)
-        sums0 = team_sums(0, both0)
-        listed = [listed0] + [gather_values(j) for j in range(1, PACK)]
-        sums1 = team_sums(1, both1)
-        val_bf = [turn_values(0, listed, "turned0", "val_rounded"), turn_values(2, listed, "sums_turned1", None)]
-        share0 = share_of(0, sums0)
-        weight0, mean0 = weight_and_mean(0, sums0, share0)
-        scaled0, centred0 = factors(0, both0, ta0, weight0, mean0)
-        share1 = share_of(1, sums1)
-        weight1, mean1 = weight_and_mean(1, sums1, share1)
-        scaled1, centred1 = factors(1, both1, ta1, weight1, mean1)
-        w_bf0 = product(0, scaled0, centred0, "val_pool3_0")
-        val_mx = [quantize("val0", val_bf[0], "mean1")]
-        w0 = quantize("w0", w_bf0)
-        w_bf1 = product(1, scaled1, centred1, "centred0")
+        a_banks = [scores("score%d" % h, q_codes[:, block(h)], q_scales[:, block(h)]) for h in range(HALVES)]
+        ta_banks = [scores("tangent%d" % h, dq_codes[:, block(h)], dq_scales[:, block(h)]) for h in range(HALVES)]
+        p_exp = sb("p_exp", full_shape, F32)
+        for h in range(HALVES):
+            nc.scalar.activation(p_exp[:, :, h], a_banks[h], EXP)
+        den = team_sums("den", [reserve_wide[:].rearrange("p g t -> p (g t)")], p_exp, None)
+        listed = [gather_values(0)]
+        tp = sb("tp", full_shape, F32, reuse="val_pool0_0")
+        for h in range(HALVES):
+            nc.vector.tensor_tensor(tp[:, :, h], ta_banks[h], p_exp[:, :, h], MULT)
+        listed.extend(gather_values(j) for j in range(1, PACK))
+        tp_sum = team_sums("tp_sum", [], tp, "val_pool2_0")
+        val_bf = [turn_values(0, listed, "tp_sum_turned", "val_rounded"), turn_values(2, listed, "den_turned", None)]
+
+        share = sb("share", [P, P], F32, reuse="val_pool1_0")
+        nc.vector.reciprocal(share[:], den[:])
+        weight = sb("weight", team_shape, F32)
+        nc.vector.tensor_tensor(weight[:].rearrange("p h g t -> p (h g) t"),
+                                share[:].rearrange("p (g t) -> p g t", t=PACK),
+                                slot_factor[:].unsqueeze(1).to_broadcast([P, G, PACK]), MULT)
+        mean = sb("mean", team_shape, F32)
+        nc.vector.tensor_tensor(mean[:].rearrange("p h g t -> p (h g t)"), tp_sum[:], share[:], MULT)
+
+        scaled = [sb("scaled%d" % h, half_shape, F32) for h in range(HALVES)]
+        centred = [sb("centred%d" % h, half_shape, F32) for h in range(HALVES)]
+        for h in range(HALVES):
+            nc.gpsimd.tensor_tensor(scaled[h][:], p_exp[:, :, h], weight[:, h].unsqueeze(1).to_broadcast(half_shape),
+                                    MULT)
+            nc.vector.tensor_tensor(centred[h][:], ta_banks[h], mean[:, h].unsqueeze(1).to_broadcast(half_shape), SUB)
+        w_bf0 = round_weights(0, scaled[0], centred[0], "val_pool3_0")
+        val_mx = [quantize("val0", val_bf[0], "mean")]
+        w_mx0 = quantize("w0", w_bf0)
+        w_bf1 = round_weights(1, scaled[1], centred[1], "centred0")
         val_mx.append(quantize("val2", val_bf[1]))
-        w1 = quantize("w1", w_bf1)
-        acc0 = read_values(0, w0[0], w0[1])
-        acc1 = read_values(1, w1[0], w1[1])
-        result_bf0 = round_result(0, acc0)
+        w_mx1 = quantize("w1", w_bf1)
+
+        acc0 = read_values(0, *w_mx0)
+        acc1 = read_values(1, *w_mx1)
+        result_bf0 = sb("result_bf0", [P, P, PACK], BF16)
+        nc.vector.tensor_copy(result_bf0[:].rearrange("p (g r) j -> p g r j", r=TEAM),
+                              acc0[:].rearrange("p j (r g) -> p g r j", r=TEAM))
         result1 = store_result(1, acc1)
-        planes(0, result_bf0)
+        store_words(0, result_bf0)
         result_bf1 = sb("result_bf1", [P, P, PACK], BF16)
-        nc.vector.tensor_copy(result_bf1[:].rearrange("p (c i) j -> p c j i", i=4),
-                              result1[:].rearrange("p j (c i) -> p c j i", i=4))
+        nc.vector.tensor_copy(*interleaved(result_bf1, result1))
         store_result(0, acc0)
-        planes(1, result_bf1)
-        for quad in range(4):
+        store_words(1, result_bf1)
+        for quad in range(QUADS):
             queue = nc.scalar if quad % 2 else nc.sync
-            queue.dma_start(out_2[0].bitcast(I32)[4 * quad : 4 * quad + 4, :],
-                            out_scales[:].bitcast(I32)[32 * quad : 32 * quad + 4, :])
+            queue.dma_start(out_2[0].bitcast(I32)[ROWS * quad : ROWS * (quad + 1), :],
+                            out_scales[:].bitcast(I32)[QUAD * quad : QUAD * quad + ROWS, :])

from contextlib import ExitStack

import concourse.mybir as mybir
from concourse.masks import make_identity

D, E, T, I, Q, G = 512, 512, 2048, 512, 256, 32
FLOPS = 2 * (2 * D * I * Q) + 2 * I * E * Q

F32 = mybir.dt.float32
BF16 = mybir.dt.bfloat16
I32 = mybir.dt.int32
U32 = mybir.dt.uint32
U16 = mybir.dt.uint16
U8 = mybir.dt.uint8
FP8X4 = mybir.dt.float8_e4m3fn_x4
FP4X4 = mybir.dt.float4_e2m1fn_x4
MULT = mybir.AluOpType.mult
SUB = mybir.AluOpType.subtract
COPY = mybir.ActivationFunctionType.Copy
EXP = mybir.ActivationFunctionType.Exp

P = 128
PACK = 4
TEAM = Q // G
HALVES = Q // P
HG = G // HALVES
QUADS, QUAD = 4, 32
ROWS = 4
LIST_GROUP = 16
RUN = 4
ON_SCALAR = 2


def tile_attend_ttteamshares_pl_kernel(tc, query, dquery, keys_words, keys_scales, reserve, factor, vals, offs,
                                        out_0, out_1, out_2):
    nc = tc.nc
    with ExitStack() as ctx:
        held = ctx.enter_context(tc.tile_pool(name="held", bufs=1))
        psum = ctx.enter_context(tc.psum_pool(name="psum", bufs=1))

        def sb(name, shape, dtype, reuse=None):
            return held.tile(shape, dtype, name=name, tag=reuse or name, align_bytes=64)

        def bank(name, shape, reuse=None):
            return psum.tile(shape, F32, name=name, tag=reuse or name)

        offsets = held.tile([P, I // LIST_GROUP], U16, name="offsets")
        key_pool = sb("key_pool", [P, T], U16)
        key_scale_pool = sb("key_scale_pool", [P, T], U8)
        nc.gpsimd.memset(key_scale_pool[:].bitcast(I32), 0)
        nc.sync.dma_start(offsets[:], offs)
        nc.sync.dma_start(key_pool[:].bitcast(I32), keys_words[0].bitcast(I32))
        for quad in range(QUADS):
            nc.sync.dma_start(key_scale_pool[:].bitcast(I32)[QUAD * quad : QUAD * quad + ROWS, :],
                              keys_scales[0].bitcast(I32)[ROWS * quad : ROWS * (quad + 1), :])
        q_raw = [sb("q_raw%d" % n, [P, PACK, Q], F32) for n in range(2)]
        for n, src in enumerate((query, dquery)):
            nc.sync.dma_start(q_raw[n][:], src.rearrange("(p t) q -> p t q", t=PACK))
        slot_reserve = sb("slot_reserve", [P, PACK], F32)
        slot_factor = sb("slot_factor", [P, PACK], F32)
        nc.sync.dma_start(slot_reserve[:], reserve.rearrange("(p t) o -> p (t o)", t=PACK))
        nc.sync.dma_start(slot_factor[:], factor.rearrange("(p t) o -> p (t o)", t=PACK))
        val_rows = vals.rearrange("(p j) t -> j p t", j=PACK)
        val_pool = []
        for j in range(PACK):
            width = T // 2 if j == ON_SCALAR else T
            parts = [sb("val_pool%d_%d" % (j, n), [P, width], F32) for n in range(T // width)]
            for n, part in enumerate(parts):
                nc.sync.dma_start(part[:], val_rows[j][:, width * n : width * (n + 1)])
            val_pool.append(parts)

        identity = sb("identity", [P, P], F32)
        make_identity(nc, identity[:])
        reserve_wide = sb("reserve_wide", [P, G, PACK], F32)
        nc.gpsimd.tensor_copy(reserve_wide[:], slot_reserve[:].unsqueeze(1).to_broadcast([P, G, PACK]))

        key_listed = sb("key_listed", [P, I], U16)
        key_words = sb("key_words", [P, PACK, P], U16)
        scale_listed = sb("scale_listed", [P, I], U8)
        key_scales = sb("key_scales", [P, PACK, P], U8)
        nc.vector.tensor_copy(key_listed[:], key_pool[:].indirect(offsets[:]))
        nc.vector.tensor_copy(scale_listed[:], key_scale_pool[:].indirect(offsets[:]))
        nc.vector.tensor_copy(key_words[:], key_listed[:].rearrange("p (s t) -> p t s", t=PACK))
        nc.vector.tensor_copy(key_scales[:], scale_listed[:].rearrange("p (s t) -> p t s", t=PACK))

        def interleaved(grouped, rows):
            return (grouped[:].rearrange("p (c i) t -> p c t i", i=RUN),
                    rows[:].rearrange("p t (c i) -> p c t i", i=RUN))

        def round_queries(name, raw):
            grouped = sb(name, [P, Q, PACK], BF16)
            nc.scalar.activation(*interleaved(grouped, raw), COPY)
            return grouped

        def quantize(name, grouped, reuse=None):
            width = grouped.shape[1]
            codes = sb(name + "_codes", [P, width], U32, reuse=reuse)
            scales = sb(name + "_scales", [P, width], U8)
            nc.vector.quantize_mx(codes[:].bitcast(FP8X4), scales[:], grouped[:].rearrange("p c t -> p (c t)"))
            return codes, scales

        def scores(name, codes, scales):
            acc = bank(name, [P, PACK, P])
            for t in range(PACK):
                nc.tensor.matmul_mx(out=acc[:, t, :], lhsT=key_words[:, t, :].bitcast(FP4X4),
                                    lhsT_scale=key_scales[:, t, :], rhs=codes.bitcast(FP8X4),
                                    rhs_scale=scales, start=True, stop=True)
            return acc[:].rearrange("p t (g r) -> p r g t", r=TEAM)

        def block(n):
            return slice(P * n, P * (n + 1))

        q_bf = round_queries("q_bf", q_raw[0])
        dq_bf = round_queries("dq_bf", q_raw[1])
        q_codes, q_scales = quantize("q", q_bf)
        dq_codes, dq_scales = quantize("dq", dq_bf)

        def gather_values(j):
            listed = sb("val_listed%d" % j, [P, I], BF16)
            if j != ON_SCALAR:
                nc.vector.tensor_copy(listed[:], val_pool[j][0][:].indirect(offsets[:]))
            else:
                rounded = sb("val_rounded", [P, T], BF16)
                for c0 in range(0, T, I):
                    n, start = divmod(c0, T // 2)
                    nc.scalar.activation(rounded[:, c0 : c0 + I], val_pool[j][n][:, start : start + I], COPY)
                nc.scalar.activation(listed[:], rounded[:].indirect(offsets[:]), COPY)
            return listed

        def turn_values(first, listed, bank_reuse, sb_reuse):
            turned = bank("turned%d" % first, [P, 2, 2, P], reuse=bank_reuse)
            for n in range(2):
                pairs = listed[first + n][:].bitcast(F32)
                for u in range(2):
                    nc.tensor.transpose(turned[:, n, u, :], pairs[:, u : 2 * P : 2], identity[:])
            grouped = sb("val_bf%d" % first, [P, 2 * P, PACK], BF16, reuse=sb_reuse)
            nc.scalar.copy(grouped[:].bitcast(F32).rearrange("p (n e) u -> p n e u", n=2),
                           turned[:].rearrange("p n u e -> p n e u"))
            return grouped

        def team_sums(name, first_terms, rows, sb_reuse):
            terms = first_terms + [rows[:, r].rearrange("p h g t -> p (h g t)") for r in range(TEAM)]
            turned = bank(name + "_turned", [P, P])
            for n, term in enumerate(terms):
                nc.tensor.matmul(turned[:], lhsT=term, rhs=identity[:], is_transpose=True,
                                 start=(n == 0), stop=(n == len(terms) - 1))
            turned_sb = sb(name + "_turned_sb", [P, P], F32, reuse=sb_reuse)
            nc.scalar.copy(turned_sb[:], turned[:])
            sums = bank(name, [P, P])
            nc.tensor.transpose(sums[:], turned_sb[:], identity[:])
            return sums

        team_shape = [P, HALVES, HG, PACK]
        half_shape = [P, TEAM, HG, PACK]
        full_shape = [P, TEAM, HALVES, HG, PACK]

        def round_weights(h, scaled, centred, reuse):
            grouped = sb("w_bf%d" % h, [P, TEAM * HG, PACK], BF16, reuse=reuse)
            nc.vector.tensor_tensor(grouped[:].rearrange("p n t -> p (n t)"),
                                    centred[:].rearrange("p r g t -> p (r g t)"),
                                    scaled[:].rearrange("p r g t -> p (r g t)"), MULT)
            return grouped

        out_codes = sb("out_codes", [P, Q], U32)
        out_scales = sb("out_scales", [P, Q], U8)
        out_words = out_1[0].rearrange("p c r -> p (c r)").bitcast(I32)
        out_rows = out_0.rearrange("(p j) q -> p j q", j=PACK)

        def read_values(h, w_codes, w_scales):
            acc = bank("out%d" % h, [P, PACK, P], reuse="score%d" % h)
            for j in range(PACK):
                val_codes, val_scales = val_mx[j // 2]
                nc.tensor.matmul_mx(out=acc[:, j, :], lhsT=val_codes[:, block(j % 2)].bitcast(FP8X4),
                                    lhsT_scale=val_scales[:, block(j % 2)], rhs=w_codes[:].bitcast(FP8X4),
                                    rhs_scale=w_scales[:], start=True, stop=True)
            return acc

        def store_result(h, acc):
            result = sb("result%d" % h, [P, PACK, P], F32)
            nc.scalar.copy(result[:].rearrange("p j (g r) -> p j g r", r=TEAM),
                           acc[:].rearrange("p j (r g) -> p j g r", r=TEAM))
            nc.sync.dma_start(out_rows[:, :, block(h)], result[:])
            return result

        def store_words(h, result_bf):
            nc.vector.quantize_mx(out_codes[:, block(h)].bitcast(FP8X4), out_scales[:, block(h)],
                                  result_bf[:].rearrange("p q j -> p (q j)"))
            nc.sync.dma_start(out_words[:, block(h)], out_codes[:, block(h)].bitcast(I32))

        a_banks = [scores("score%d" % h, q_codes[:, block(h)], q_scales[:, block(h)]) for h in range(HALVES)]
        ta_banks = [scores("tangent%d" % h, dq_codes[:, block(h)], dq_scales[:, block(h)]) for h in range(HALVES)]
        p_exp = sb("p_exp", full_shape, F32)
        for h in range(HALVES):
            nc.scalar.activation(p_exp[:, :, h], a_banks[h], EXP)
        den = team_sums("den", [reserve_wide[:].rearrange("p g t -> p (g t)")], p_exp, None)
        listed = [gather_values(0)]
        tp = sb("tp", full_shape, F32, reuse="val_pool0_0")
        for h in range(HALVES):
            nc.vector.tensor_tensor(tp[:, :, h], ta_banks[h], p_exp[:, :, h], MULT)
        listed.extend(gather_values(j) for j in range(1, PACK))
        tp_sum = team_sums("tp_sum", [], tp, "val_pool2_0")
        val_bf = [turn_values(0, listed, "tp_sum_turned", "val_rounded"), turn_values(2, listed, "den_turned", None)]

        share = sb("share", [P, P], F32, reuse="val_pool1_0")
        nc.vector.reciprocal(share[:], den[:])
        weight = sb("weight", team_shape, F32)
        nc.vector.tensor_tensor(weight[:].rearrange("p h g t -> p (h g) t"),
                                share[:].rearrange("p (g t) -> p g t", t=PACK),
                                slot_factor[:].unsqueeze(1).to_broadcast([P, G, PACK]), MULT)
        mean = sb("mean", team_shape, F32)
        nc.vector.tensor_tensor(mean[:].rearrange("p h g t -> p (h g t)"), tp_sum[:], share[:], MULT)

        scaled = [sb("scaled%d" % h, half_shape, F32) for h in range(HALVES)]
        centred = [sb("centred%d" % h, half_shape, F32) for h in range(HALVES)]
        for h in range(HALVES):
            nc.gpsimd.tensor_tensor(scaled[h][:], p_exp[:, :, h], weight[:, h].unsqueeze(1).to_broadcast(half_shape),
                                    MULT)
            nc.vector.tensor_tensor(centred[h][:], ta_banks[h], mean[:, h].unsqueeze(1).to_broadcast(half_shape), SUB)
        w_bf0 = round_weights(0, scaled[0], centred[0], "val_pool3_0")
        val_mx = [quantize("val0", val_bf[0], "mean")]
        w_mx0 = quantize("w0", w_bf0)
        w_bf1 = round_weights(1, scaled[1], centred[1], "centred0")
        val_mx.append(quantize("val2", val_bf[1]))
        w_mx1 = quantize("w1", w_bf1)

        acc0 = read_values(0, *w_mx0)
        acc1 = read_values(1, *w_mx1)
        result_bf0 = sb("result_bf0", [P, P, PACK], BF16)
        nc.vector.tensor_copy(result_bf0[:].rearrange("p (g r) j -> p g r j", r=TEAM),
                              acc0[:].rearrange("p j (r g) -> p g r j", r=TEAM))
        result1 = store_result(1, acc1)
        store_words(0, result_bf0)
        result_bf1 = sb("result_bf1", [P, P, PACK], BF16)
        nc.vector.tensor_copy(*interleaved(result_bf1, result1))
        store_result(0, acc0)
        store_words(1, result_bf1)
        for quad in range(QUADS):
            queue = nc.scalar if quad % 2 else nc.sync
            queue.dma_start(out_2[0].bitcast(I32)[ROWS * quad : ROWS * (quad + 1), :],
                            out_scales[:].bitcast(I32)[QUAD * quad : QUAD * quad + ROWS, :])
